import numpy as np
import ml_dtypes


def mxq(x, axis, fmt="e4m3"):
    dtype, down = {"e4m3": (ml_dtypes.float8_e4m3fn, 7), "e5m2": (ml_dtypes.float8_e5m2, 14)}[fmt]
    v = np.moveaxis(np.asarray(x, np.float32).astype(ml_dtypes.bfloat16).astype(np.float64), axis, -1)
    blocks = v.reshape(v.shape[:-1] + (-1, 32))
    amax = np.abs(blocks).max(-1, keepdims=True)
    byte = np.maximum(np.where(amax > 0, np.frexp(amax)[1] - 1 + 127, 0) - down, 1)
    scale = np.exp2(byte - 127.0)
    codes = (blocks / scale).astype(np.float32).astype(dtype).astype(np.float64)
    return np.moveaxis((codes * scale).reshape(v.shape), -1, axis)


WIDE = False


def mx_kscale(k):
    if not WIDE:
        return np.ones(k)
    levels = np.array([10, -10, 5, -5, 0])
    if k % 512:
        return np.exp2(np.random.permutation(np.resize(levels, k // 32))).repeat(32)
    a = np.empty((k // 512, 16))
    for p in range(k // 512):
        a[p, :8] = np.random.permutation(np.resize(levels, 8))
        for g in range(8):
            far = levels[np.abs(levels - a[p, g]) >= 10]
            a[p, g + 8] = far[np.random.randint(len(far))]
    return np.exp2(a.ravel()).repeat(32)


def f64(x):
    return np.asarray(x).astype(np.float64)


def striped(idx):
    return np.tile(idx.reshape(-1, 16).T, (8, 1)).astype(np.uint16)


def unstriped(offs):
    return offs[:16].T.reshape(-1).astype(np.int64)


def pack_weight(w):
    k, n = w.shape
    w = f64(np.asarray(w, np.float32).astype(ml_dtypes.bfloat16)).reshape(k // 32, 32, n)
    amax = np.abs(w).max(1)
    byte = np.clip(np.where(amax > 0, np.frexp(amax)[1] - 1 + 127 - 7, 1), 1, 254)
    scaled = (w * np.exp2(127.0 - byte)[:, None, :]).reshape(k, n).astype(np.float32)
    words = np.ascontiguousarray(scaled.reshape(k // 512, 128, 4, n).transpose(0, 1, 3, 2)).astype(ml_dtypes.float8_e4m3fn).view(np.uint8)
    return words, np.ascontiguousarray(byte.astype(np.uint8).reshape(k // 512, 16, n))


def unpack_weight(words, scales):
    g, p, n, _ = words.shape
    vals = np.ascontiguousarray(words).view(ml_dtypes.float8_e4m3fn).astype(np.float64) * np.repeat(np.exp2(scales.astype(np.float64) - 127.0), 8, axis=1)[..., None]
    return vals.transpose(0, 1, 3, 2).reshape(g * 512, n)


K, T, S, V, N = 1024, 1024, 512, 256, 128


def setup_inputs():
    n = np.random.standard_normal
    s = mx_kscale(K)[:, None]
    packed_w1 = pack_weight(n((K, N)) / np.sqrt(K) / s)
    return {
        "xT": (n((K, T)) * s).astype(np.float32),
        "w1_words": packed_w1[0],
        "w1_scales": packed_w1[1],
        "offs": striped(np.random.permutation(T)[:S]),
        "pos1": striped(np.random.permutation(S)[:V]),
        "pos2": striped(np.random.permutation(S)[:V]),
        "pos3": striped(np.random.permutation(S)[:V]),
    }


def reference(xT, w1_words, w1_scales, offs, pos1, pos2, pos3):
    xq = mxq(f64(xT)[:, unstriped(offs)], 0, "e4m3")
    y = unpack_weight(w1_words, w1_scales).T @ xq
    n0 = y[:, unstriped(pos1)]
    n1 = y[:, unstriped(pos2)]
    n2 = y[:, unstriped(pos3)]
    return np.maximum(np.minimum(n0, n1), np.minimum(np.maximum(n0, n1), n2))

@@ -1,0 +1,164 @@
+from contextlib import ExitStack
+
+import concourse.mybir as mybir
+
+K, T, S, V, N = 1024, 1024, 512, 256, 128
+FLOPS = 2 * K * N * S
+
+F32 = mybir.dt.float32
+BF16 = mybir.dt.bfloat16
+I32 = mybir.dt.int32
+U32 = mybir.dt.uint32
+U16 = mybir.dt.uint16
+U8 = mybir.dt.uint8
+FP8X4 = mybir.dt.float8_e4m3fn_x4
+MAX = mybir.AluOpType.max
+MIN = mybir.AluOpType.min
+
+P = 128
+K_PASS = 512
+PASSES = K // K_PASS
+LIST_ROWS = 16
+
+LOADS = [
+    (0, 0, 512, 0), (0, 512, 1024, 352),
+    (1, 0, 512, 0), (1, 512, 1024, 352),
+    (2, 0, 512, 0), (2, 512, 1024, 0),
+    (3, 0, 384, 0), (3, 384, 768, 0), (3, 768, 1024, 256),
+]
+PIECES = [(0, 256), (256, 512)]
+
+
+def tile_picked_median_none_e_kernel(
+    tc, xT, w1_words, w1_scales, offs, pos1, pos2, pos3, out
+):
+    nc = tc.nc
+    with ExitStack() as ctx:
+        keep = ctx.enter_context(tc.tile_pool(name="keep", bufs=1))
+        psum = ctx.enter_context(tc.psum_pool(name="psum", bufs=1))
+
+        picked = keep.tile([P, S // LIST_ROWS], U16, name="picked")
+        places = [keep.tile([P, V // LIST_ROWS], U16, name=f"places{d}") for d in range(3)]
+        w_codes = keep.tile([P, PASSES, N], U32, name="w_codes", align_bytes=64)
+        w_scales = keep.tile([P, PASSES, N], U8, name="w_scales", align_bytes=64)
+        nc.gpsimd.memset(w_scales[:], 0)
+
+        raws = []
+        for i, (pair, c0, c1, v_cols) in enumerate(LOADS):
+            z, u = divmod(pair, 2)
+            rows = xT[z * K_PASS : (z + 1) * K_PASS, :].rearrange("(p j) t -> p j t", j=4)
+            raw = keep.tile([P, 2, c1 - c0], F32, name=f"raw{i}")
+            nc.sync.dma_start(out=raw[:], in_=rows[:, 2 * u : 2 * u + 2, c0:c1])
+            raws.append(raw)
+            if i == 0:
+                nc.sync.dma_start(picked[:], offs)
+
+        nc.sync.dma_start(
+            out=w_codes[:].bitcast(I32),
+            in_=w1_words.rearrange("z p n t -> p z (n t)").bitcast(I32),
+        )
+        for r in range(4):
+            nc.gpsimd.dma_start(
+                out=w_scales[r:P:32, :, :].bitcast(I32),
+                in_=w1_scales[:, r:16:4, :].rearrange("z q n -> q z n").bitcast(I32),
+            )
+        for tile, pos in zip(places, (pos1, pos2, pos3)):
+            nc.sync.dma_start(tile[:], pos)
+
+        pairs = [keep.tile([P, T, 2], BF16, name=f"pairs{q}") for q in range(4)]
+        fetched = {1: keep.tile([P, 2, S], U32, name="fetched1")}
+
+        def cast(i):
+            pair, c0, c1, v_cols = LOADS[i]
+            src = raws[i][:].rearrange("p e t -> p t e")
+            if v_cols:
+                nc.vector.tensor_copy(out=pairs[pair][:, c0 : c0 + v_cols, :], in_=src[:, :v_cols, :])
+            if c0 + v_cols < c1:
+                nc.scalar.copy(out=pairs[pair][:, c0 + v_cols : c1, :], in_=src[:, v_cols:, :])
+
+        def gather(pair, s0, s1):
+            z, u = divmod(pair, 2)
+            window = pairs[pair][:].rearrange("p t e -> p (t e)").bitcast(U32)
+            nc.vector.tensor_copy(
+                out=fetched[z][:, u, s0:s1],
+                in_=window.indirect(picked[:, s0 // LIST_ROWS : s1 // LIST_ROWS]),
+            )
+
+        woven0 = keep.tile([P, 4 * S], BF16, name="woven0", align_bytes=64)
+
+        def gather_woven(pair):
+            window = pairs[pair][:].rearrange("p t e -> p (t e)").bitcast(U32)
+            dst = woven0[:].bitcast(U32).rearrange("p (s u) -> p s u", u=2)
+            nc.vector.tensor_copy(out=dst[:, :, pair], in_=window.indirect(picked[:]))
+
+        def weave(z, s0, s1, on_vector):
+            woven = keep.tile([P, 4 * (s1 - s0)], BF16, name=f"woven{z}_{s0}", align_bytes=64)
+            src = fetched[z][:, :, s0:s1].rearrange("p u s -> p s u")
+            if on_vector:
+                dst = woven[:].bitcast(I32).rearrange("p (s u) -> p s u", u=2)
+                src = fetched[z][:].bitcast(I32)[:, :, s0:s1].rearrange("p u s -> p s u")
+                nc.vector.tensor_copy(out=dst, in_=src)
+            else:
+                dst = woven[:].bitcast(U32).rearrange("p (s u) -> p s u", u=2)
+                nc.scalar.copy(out=dst, in_=src)
+            return woven
+
+        def quantise(z, s0, s1, woven):
+            codes = keep.tile([P, s1 - s0], U32, name=f"codes{z}_{s0}", align_bytes=64)
+            scales = keep.tile([P, s1 - s0], U8, name=f"scales{z}_{s0}", align_bytes=64)
+            nc.vector.quantize_mx(out=codes[:].bitcast(FP8X4), scales=scales[:], in_=woven[:])
+            return codes, scales
+
+        def multiply(bank, z, codes, scales):
+            nc.tensor.matmul_mx(
+                out=bank[:],
+                lhsT=w_codes[:, z, :].bitcast(FP8X4),
+                lhsT_scale=w_scales[:, z, :],
+                rhs=codes.bitcast(FP8X4),
+                rhs_scale=scales,
+                start=(z == 0),
+                stop=(z == PASSES - 1),
+            )
+
+        banks = [psum.tile([N, s1 - s0], F32, name=f"bank{s0}") for s0, s1 in PIECES]
+        y = keep.tile([N, S], F32, name="y")
+
+        cast(0)
+        cast(1)
+        gather_woven(0)
+        cast(2)
+        cast(3)
+        gather_woven(1)
+        cast(4)
+        codes0, scales0 = quantise(0, 0, S, woven0)
+        cast(5)
+        gather(2, 0, S)
+        cast(6)
+        cast(7)
+        cast(8)
+        for bank, (s0, s1) in zip(banks, PIECES):
+            multiply(bank, 0, codes0[:, s0:s1], scales0[:, s0:s1])
+        for s0, s1 in PIECES:
+            gather(3, s0, s1)
+        wovens = [weave(1, s0, s1, False) for s0, s1 in PIECES]
+        for bank, woven, (s0, s1) in zip(banks, wovens, PIECES):
+            codes, scales = quantise(1, s0, s1, woven)
+            multiply(bank, 1, codes[:], scales[:])
+        for bank, (s0, s1) in zip(banks, PIECES):
+            nc.scalar.copy(out=y[:, s0:s1], in_=bank[:])
+
+        near = [keep.tile([N, V], F32, name=f"near{d}") for d in range(3)]
+        for d in range(3):
+            nc.vector.tensor_copy(out=near[d][:], in_=y[:].indirect(places[d][:]))
+        high = keep.tile([N, V], F32, name="high")
+        low = keep.tile([N, V], F32, name="low")
+        capped = keep.tile([N, V], F32, name="capped")
+        median = keep.tile([N, V], F32, name="median")
+        nc.vector.tensor_tensor(high[:], near[0][:], near[1][:], MAX)
+        nc.vector.tensor_tensor(low[:], near[0][:], near[1][:], MIN)
+        halves = [slice(0, V // 2), slice(V // 2, V)]
+        for h in halves:
+            nc.vector.tensor_tensor(capped[:, h], high[:, h], near[2][:, h], MIN)
+        for h in halves:
+            nc.vector.tensor_tensor(median[:, h], low[:, h], capped[:, h], MAX)
+        nc.sync.dma_start(out=out, in_=median[:])

@@ -21,12 +21,12 @@ PASSES = K // K_PASS
 LIST_ROWS = 16
 
 LOADS = [
-    (0, 0, 512, 0), (0, 512, 1024, 352),
-    (1, 0, 512, 0), (1, 512, 1024, 352),
+    (0, 0, 1024, 688),
+    (1, 0, 1024, 576),
     (2, 0, 512, 0), (2, 512, 1024, 0),
     (3, 0, 384, 0), (3, 384, 768, 0), (3, 768, 1024, 256),
 ]
-PIECES = [(0, 256), (256, 512)]
+PIECES = [(0, 128), (128, 256), (256, 384), (384, 512)]
 
 
 def tile_picked_median_none_e_kernel(
@@ -41,7 +41,7 @@ def tile_picked_median_none_e_kernel(
         places = [keep.tile([P, V // LIST_ROWS], U16, name=f"places{d}") for d in range(3)]
         w_codes = keep.tile([P, PASSES, N], U32, name="w_codes", align_bytes=64)
         w_scales = keep.tile([P, PASSES, N], U8, name="w_scales", align_bytes=64)
-        nc.gpsimd.memset(w_scales[:], 0)
+        nc.vector.memset(w_scales[:].bitcast(I32), 0)
 
         raws = []
         for i, (pair, c0, c1, v_cols) in enumerate(LOADS):
@@ -58,7 +58,7 @@ def tile_picked_median_none_e_kernel(
             in_=w1_words.rearrange("z p n t -> p z (n t)").bitcast(I32),
         )
         for r in range(4):
-            nc.gpsimd.dma_start(
+            nc.sync.dma_start(
                 out=w_scales[r:P:32, :, :].bitcast(I32),
                 in_=w1_scales[:, r:16:4, :].rearrange("z q n -> q z n").bitcast(I32),
             )
@@ -124,18 +124,16 @@ def tile_picked_median_none_e_kernel(
         y = keep.tile([N, S], F32, name="y")
 
         cast(0)
-        cast(1)
         gather_woven(0)
-        cast(2)
-        cast(3)
+        cast(1)
         gather_woven(1)
-        cast(4)
+        cast(2)
         codes0, scales0 = quantise(0, 0, S, woven0)
-        cast(5)
+        cast(3)
         gather(2, 0, S)
+        cast(4)
+        cast(5)
         cast(6)
-        cast(7)
-        cast(8)
         for bank, (s0, s1) in zip(banks, PIECES):
             multiply(bank, 0, codes0[:, s0:s1], scales0[:, s0:s1])
         for s0, s1 in PIECES:
@@ -159,6 +157,6 @@ def tile_picked_median_none_e_kernel(
         halves = [slice(0, V // 2), slice(V // 2, V)]
         for h in halves:
             nc.vector.tensor_tensor(capped[:, h], high[:, h], near[2][:, h], MIN)
-        for h in halves:
+        for h, queue in zip(halves, (nc.sync, nc.scalar)):
             nc.vector.tensor_tensor(median[:, h], low[:, h], capped[:, h], MAX)
-        nc.sync.dma_start(out=out, in_=median[:])
+            queue.dma_start(out=out[:, h], in_=median[:, h])

@@ -21,11 +21,12 @@ PASSES = K // K_PASS
 LIST_ROWS = 16
 
 LOADS = [
-    (0, 0, 1024, 688),
-    (1, 0, 1024, 576),
+    (0, 0, 512, 0), (0, 512, 1024, 352),
+    (1, 0, 512, 0), (1, 512, 1024, 352),
     (2, 0, 512, 0), (2, 512, 1024, 0),
     (3, 0, 384, 0), (3, 384, 768, 0), (3, 768, 1024, 256),
 ]
+HALVES = [(0, 256), (256, 512)]
 PIECES = [(0, 128), (128, 256), (256, 384), (384, 512)]
 
 
@@ -66,7 +67,7 @@ def tile_picked_median_none_e_kernel(
             nc.sync.dma_start(tile[:], pos)
 
         pairs = [keep.tile([P, T, 2], BF16, name=f"pairs{q}") for q in range(4)]
-        fetched = {1: keep.tile([P, 2, S], U32, name="fetched1")}
+        fetched = [keep.tile([P, 2, S], U32, name=f"fetched{z}") for z in range(PASSES)]
 
         def cast(i):
             pair, c0, c1, v_cols = LOADS[i]
@@ -83,13 +84,6 @@ def tile_picked_median_none_e_kernel(
                 out=fetched[z][:, u, s0:s1],
                 in_=window.indirect(picked[:, s0 // LIST_ROWS : s1 // LIST_ROWS]),
             )
-
-        woven0 = keep.tile([P, 4 * S], BF16, name="woven0", align_bytes=64)
-
-        def gather_woven(pair):
-            window = pairs[pair][:].rearrange("p t e -> p (t e)").bitcast(U32)
-            dst = woven0[:].bitcast(U32).rearrange("p (s u) -> p s u", u=2)
-            nc.vector.tensor_copy(out=dst[:, :, pair], in_=window.indirect(picked[:]))
 
         def weave(z, s0, s1, on_vector):
             woven = keep.tile([P, 4 * (s1 - s0)], BF16, name=f"woven{z}_{s0}", align_bytes=64)
@@ -124,18 +118,23 @@ def tile_picked_median_none_e_kernel(
         y = keep.tile([N, S], F32, name="y")
 
         cast(0)
-        gather_woven(0)
         cast(1)
-        gather_woven(1)
+        gather(0, 0, S)
         cast(2)
-        codes0, scales0 = quantise(0, 0, S, woven0)
         cast(3)
-        gather(2, 0, S)
+        for s0, s1 in HALVES:
+            gather(1, s0, s1)
         cast(4)
+        wovens0 = [weave(0, s0, s1, True) for s0, s1 in HALVES]
+        quantised0 = [quantise(0, s0, s1, woven) for woven, (s0, s1) in zip(wovens0, HALVES)]
         cast(5)
+        gather(2, 0, S)
         cast(6)
+        cast(7)
+        cast(8)
         for bank, (s0, s1) in zip(banks, PIECES):
-            multiply(bank, 0, codes0[:, s0:s1], scales0[:, s0:s1])
+            codes, scales = quantised0[s0 // 256]
+            multiply(bank, 0, codes[:, s0 % 256 : s0 % 256 + 128], scales[:, s0 % 256 : s0 % 256 + 128])
         for s0, s1 in PIECES:
             gather(3, s0, s1)
         wovens = [weave(1, s0, s1, False) for s0, s1 in PIECES]
@@ -157,6 +156,6 @@ def tile_picked_median_none_e_kernel(
         halves = [slice(0, V // 2), slice(V // 2, V)]
         for h in halves:
             nc.vector.tensor_tensor(capped[:, h], high[:, h], near[2][:, h], MIN)
-        for h, queue in zip(halves, (nc.sync, nc.scalar)):
+        for h in halves:
             nc.vector.tensor_tensor(median[:, h], low[:, h], capped[:, h], MAX)
-            queue.dma_start(out=out[:, h], in_=median[:, h])
+        nc.sync.dma_start(out=out, in_=median[:])

from contextlib import ExitStack

import concourse.mybir as mybir

K, T, S, V, N = 1024, 1024, 512, 256, 128
FLOPS = 2 * K * N * S

F32 = mybir.dt.float32
BF16 = mybir.dt.bfloat16
I32 = mybir.dt.int32
U32 = mybir.dt.uint32
U16 = mybir.dt.uint16
U8 = mybir.dt.uint8
FP8X4 = mybir.dt.float8_e4m3fn_x4
MAX = mybir.AluOpType.max
MIN = mybir.AluOpType.min

P = 128
K_PASS = 512
PASSES = K // K_PASS
LIST_ROWS = 16

LOADS = [
    (0, 0, 512, 0), (0, 512, 1024, 352),
    (1, 0, 512, 0), (1, 512, 1024, 352),
    (2, 0, 512, 0), (2, 512, 1024, 0),
    (3, 0, 384, 0), (3, 384, 768, 0), (3, 768, 1024, 256),
]
HALVES = [(0, 256), (256, 512)]
PIECES = [(0, 128), (128, 256), (256, 384), (384, 512)]


def tile_picked_median_none_e_kernel(
    tc, xT, w1_words, w1_scales, offs, pos1, pos2, pos3, out
):
    nc = tc.nc
    with ExitStack() as ctx:
        keep = ctx.enter_context(tc.tile_pool(name="keep", bufs=1))
        psum = ctx.enter_context(tc.psum_pool(name="psum", bufs=1))

        picked = keep.tile([P, S // LIST_ROWS], U16, name="picked")
        places = [keep.tile([P, V // LIST_ROWS], U16, name=f"places{d}") for d in range(3)]
        w_codes = keep.tile([P, PASSES, N], U32, name="w_codes", align_bytes=64)
        w_scales = keep.tile([P, PASSES, N], U8, name="w_scales", align_bytes=64)
        nc.vector.memset(w_scales[:].bitcast(I32), 0)

        raws = []
        for i, (pair, c0, c1, v_cols) in enumerate(LOADS):
            z, u = divmod(pair, 2)
            rows = xT[z * K_PASS : (z + 1) * K_PASS, :].rearrange("(p j) t -> p j t", j=4)
            raw = keep.tile([P, 2, c1 - c0], F32, name=f"raw{i}")
            nc.sync.dma_start(out=raw[:], in_=rows[:, 2 * u : 2 * u + 2, c0:c1])
            raws.append(raw)
            if i == 0:
                nc.sync.dma_start(picked[:], offs)

        nc.sync.dma_start(
            out=w_codes[:].bitcast(I32),
            in_=w1_words.rearrange("z p n t -> p z (n t)").bitcast(I32),
        )
        for r in range(4):
            nc.sync.dma_start(
                out=w_scales[r:P:32, :, :].bitcast(I32),
                in_=w1_scales[:, r:16:4, :].rearrange("z q n -> q z n").bitcast(I32),
            )
        for tile, pos in zip(places, (pos1, pos2, pos3)):
            nc.sync.dma_start(tile[:], pos)

        pairs = [keep.tile([P, T, 2], BF16, name=f"pairs{q}") for q in range(4)]
        fetched = [keep.tile([P, 2, S], U32, name=f"fetched{z}") for z in range(PASSES)]

        def cast(i):
            pair, c0, c1, v_cols = LOADS[i]
            src = raws[i][:].rearrange("p e t -> p t e")
            if v_cols:
                nc.vector.tensor_copy(out=pairs[pair][:, c0 : c0 + v_cols, :], in_=src[:, :v_cols, :])
            if c0 + v_cols < c1:
                nc.scalar.copy(out=pairs[pair][:, c0 + v_cols : c1, :], in_=src[:, v_cols:, :])

        def gather(pair, s0, s1):
            z, u = divmod(pair, 2)
            window = pairs[pair][:].rearrange("p t e -> p (t e)").bitcast(U32)
            nc.vector.tensor_copy(
                out=fetched[z][:, u, s0:s1],
                in_=window.indirect(picked[:, s0 // LIST_ROWS : s1 // LIST_ROWS]),
            )

        def weave(z, s0, s1, on_vector):
            woven = keep.tile([P, 4 * (s1 - s0)], BF16, name=f"woven{z}_{s0}", align_bytes=64)
            src = fetched[z][:, :, s0:s1].rearrange("p u s -> p s u")
            if on_vector:
                dst = woven[:].bitcast(I32).rearrange("p (s u) -> p s u", u=2)
                src = fetched[z][:].bitcast(I32)[:, :, s0:s1].rearrange("p u s -> p s u")
                nc.vector.tensor_copy(out=dst, in_=src)
            else:
                dst = woven[:].bitcast(U32).rearrange("p (s u) -> p s u", u=2)
                nc.scalar.copy(out=dst, in_=src)
            return woven

        def quantise(z, s0, s1, woven):
            codes = keep.tile([P, s1 - s0], U32, name=f"codes{z}_{s0}", align_bytes=64)
            scales = keep.tile([P, s1 - s0], U8, name=f"scales{z}_{s0}", align_bytes=64)
            nc.vector.quantize_mx(out=codes[:].bitcast(FP8X4), scales=scales[:], in_=woven[:])
            return codes, scales

        def multiply(bank, z, codes, scales):
            nc.tensor.matmul_mx(
                out=bank[:],
                lhsT=w_codes[:, z, :].bitcast(FP8X4),
                lhsT_scale=w_scales[:, z, :],
                rhs=codes.bitcast(FP8X4),
                rhs_scale=scales,
                start=(z == 0),
                stop=(z == PASSES - 1),
            )

        banks = [psum.tile([N, s1 - s0], F32, name=f"bank{s0}") for s0, s1 in PIECES]
        y = keep.tile([N, S], F32, name="y")

        cast(0)
        cast(1)
        gather(0, 0, S)
        cast(2)
        cast(3)
        for s0, s1 in HALVES:
            gather(1, s0, s1)
        cast(4)
        wovens0 = [weave(0, s0, s1, True) for s0, s1 in HALVES]
        quantised0 = [quantise(0, s0, s1, woven) for woven, (s0, s1) in zip(wovens0, HALVES)]
        cast(5)
        gather(2, 0, S)
        cast(6)
        cast(7)
        cast(8)
        for bank, (s0, s1) in zip(banks, PIECES):
            codes, scales = quantised0[s0 // 256]
            multiply(bank, 0, codes[:, s0 % 256 : s0 % 256 + 128], scales[:, s0 % 256 : s0 % 256 + 128])
        for s0, s1 in PIECES:
            gather(3, s0, s1)
        wovens = [weave(1, s0, s1, False) for s0, s1 in PIECES]
        for bank, woven, (s0, s1) in zip(banks, wovens, PIECES):
            codes, scales = quantise(1, s0, s1, woven)
            multiply(bank, 1, codes[:], scales[:])
        for bank, (s0, s1) in zip(banks, PIECES):
            nc.scalar.copy(out=y[:, s0:s1], in_=bank[:])

        near = [keep.tile([N, V], F32, name=f"near{d}") for d in range(3)]
        for d in range(3):
            nc.vector.tensor_copy(out=near[d][:], in_=y[:].indirect(places[d][:]))
        high = keep.tile([N, V], F32, name="high")
        low = keep.tile([N, V], F32, name="low")
        capped = keep.tile([N, V], F32, name="capped")
        median = keep.tile([N, V], F32, name="median")
        nc.vector.tensor_tensor(high[:], near[0][:], near[1][:], MAX)
        nc.vector.tensor_tensor(low[:], near[0][:], near[1][:], MIN)
        halves = [slice(0, V // 2), slice(V // 2, V)]
        for h in halves:
            nc.vector.tensor_tensor(capped[:, h], high[:, h], near[2][:, h], MIN)
        for h in halves:
            nc.vector.tensor_tensor(median[:, h], low[:, h], capped[:, h], MAX)
        nc.sync.dma_start(out=out, in_=median[:])
